import numpy as np
import ml_dtypes


def mxq(x, axis, fmt="e4m3"):
    dtype, down = {"e4m3": (ml_dtypes.float8_e4m3fn, 7), "e5m2": (ml_dtypes.float8_e5m2, 14)}[fmt]
    v = np.moveaxis(np.asarray(x, np.float32).astype(ml_dtypes.bfloat16).astype(np.float64), axis, -1)
    blocks = v.reshape(v.shape[:-1] + (-1, 32))
    amax = np.abs(blocks).max(-1, keepdims=True)
    byte = np.maximum(np.where(amax > 0, np.frexp(amax)[1] - 1 + 127, 0) - down, 1)
    scale = np.exp2(byte - 127.0)
    codes = (blocks / scale).astype(np.float32).astype(dtype).astype(np.float64)
    return np.moveaxis((codes * scale).reshape(v.shape), -1, axis)


WIDE = False


def mx_kscale(k):
    if not WIDE:
        return np.ones(k)
    levels = np.array([10, -10, 5, -5, 0])
    if k % 512:
        return np.exp2(np.random.permutation(np.resize(levels, k // 32))).repeat(32)
    a = np.empty((k // 512, 16))
    for p in range(k // 512):
        a[p, :8] = np.random.permutation(np.resize(levels, 8))
        for g in range(8):
            far = levels[np.abs(levels - a[p, g]) >= 10]
            a[p, g + 8] = far[np.random.randint(len(far))]
    return np.exp2(a.ravel()).repeat(32)


BF16 = ml_dtypes.bfloat16


def bf(x):
    return np.asarray(x, np.float32).astype(BF16)


def f64(x):
    return np.asarray(x).astype(np.float64)


E2M1 = np.array([0.0, 0.5, 1.0, 1.5, 2.0, 3.0, 4.0, 6.0, -0.0, -0.5, -1.0, -1.5, -2.0, -3.0, -4.0, -6.0])


def pack_weight(w, fmt):
    k, n = w.shape
    w = f64(bf(w)).reshape(k // 32, 32, n)
    amax = np.abs(w).max(1)
    if fmt == "e4m3":
        byte = np.frexp(amax)[1] - 1 + 127 - 7
    else:
        mant, ex = np.frexp(amax / 6.0)
        byte = np.where(mant > 0.5, ex, ex - 1) + 127
    byte = np.clip(np.where(amax > 0, byte, 1), 1, 254)
    scaled = (w * np.exp2(127.0 - byte)[:, None, :]).reshape(k, n).astype(np.float32)
    by_word = np.ascontiguousarray(scaled.reshape(k // 512, 128, 4, n).transpose(0, 1, 3, 2))
    if fmt == "e4m3":
        words = by_word.astype(ml_dtypes.float8_e4m3fn).view(np.uint8)
    else:
        c = by_word.astype(ml_dtypes.float4_e2m1fn).view(np.uint8) & 0xF
        words = c[..., 0::2] | (c[..., 1::2] << 4)
    return np.ascontiguousarray(words), np.ascontiguousarray(byte.astype(np.uint8).reshape(k // 512, 16, n))


def unpack_weight(words, scales, fmt):
    g, p, n, _ = words.shape
    if fmt == "e4m3":
        vals = np.ascontiguousarray(words).view(ml_dtypes.float8_e4m3fn).astype(np.float64)
    else:
        nib = np.empty((g, p, n, 4), np.uint8)
        nib[..., 0::2] = words & 0xF
        nib[..., 1::2] = words >> 4
        vals = E2M1[nib]
    vals = vals * np.repeat(np.exp2(scales.astype(np.float64) - 127.0), 8, axis=1)[..., None]
    return vals.transpose(0, 1, 3, 2).reshape(g * 512, n)
def pack4(w):
    words, scales = pack_weight(w, "e2m1")
    return words.reshape(words.shape[0], 128, -1), scales


def unpack4(words, scales):
    return unpack_weight(words.reshape(words.shape[0], 128, -1, 2), scales, "e2m1")


E4M3FN = np.array([(-1.0 if i & 128 else 1.0) * ((1.0 + (i & 7) / 8.0) * 2.0 ** (((i >> 3) & 15) - 7) if i & 120 else (i & 7) * 2.0 ** -9) for i in range(256)])


def e4m3fn_bytes(y):
    return np.clip(np.asarray(y, np.float64), -448.0, 448.0).astype(np.float32).astype(ml_dtypes.float8_e4m3fn).view(np.uint8)


def e4m3fn_values(b):
    return E4M3FN[b]


T, D, C = 2048, 1024, 1024


def softplus(a):
    return np.maximum(a, 0.0) + np.log1p(np.exp(-np.abs(a)))


def draw0():
    s, t = mx_kscale(D), mx_kscale(C)
    x = bf(np.random.standard_normal((T, D)) * s)
    w_words, w_scales = pack4(np.random.standard_normal((D, C)) / np.sqrt(D) / s[:, None])
    p = bf((1.0 + 0.3 * np.random.standard_normal(C)) * t)
    gamma_words, gamma_scales = pack4(np.random.standard_normal((C, C)) / np.sqrt(C) / t[:, None])
    beta = bf(1.0 + 0.5 * np.random.standard_normal(C))
    return {"x": x,
            "w_words": w_words,
            "w_scales": w_scales,
            "p": p,
            "gamma_words": gamma_words,
            "gamma_scales": gamma_scales,
            "beta": beta}


def core(x, w_words, w_scales, p, gamma_words, gamma_scales, beta):
    y = mxq(f64(x), 1, "e4m3") @ unpack4(w_words, w_scales)
    q = (y * y - 1.0) * f64(p)[None, :]
    pool = f64(beta)[None, :] + (mxq(q, 1, "e4m3") @ unpack4(gamma_words, gamma_scales))
    den = np.sqrt(0.1 + softplus(pool))
    return y / den


def setup_inputs():
    drawn = draw0()
    full = np.asarray(drawn['x']).astype(np.float64)
    scale = (np.abs(full).reshape(2048, 8, 128).max(axis=(2,)) / 448.0).astype(np.float32)
    given = {}
    for key, value in drawn.items():
        if key == 'x':
            given['x_bytes'] = e4m3fn_bytes(full / np.repeat(scale.astype(np.float64), 128, axis=1))
            given['x_scale'] = scale
        else:
            given[key] = value
    return given


def reference(x_bytes, x_scale, w_words, w_scales, p, gamma_words, gamma_scales, beta):
    return core(e4m3fn_values(x_bytes) * np.repeat(x_scale.astype(np.float64), 128, axis=1), w_words, w_scales, p, gamma_words, gamma_scales, beta)

@@ -1,0 +1,265 @@
+from contextlib import ExitStack
+
+import concourse.mybir as mybir
+from concourse.masks import make_identity
+
+T, D, C = 2048, 1024, 1024
+FLOPS = 2 * T * D * C + 2 * T * C * C
+
+F32 = mybir.dt.float32
+BF16 = mybir.dt.bfloat16
+U32 = mybir.dt.uint32
+I32 = mybir.dt.int32
+U8 = mybir.dt.uint8
+FP8 = mybir.dt.float8_e4m3fn
+FP8X4 = mybir.dt.float8_e4m3fn_x4
+FP4X4 = mybir.dt.float4_e2m1fn_x4
+ALU = mybir.AluOpType
+ACT = mybir.ActivationFunctionType
+
+P = 128
+TILES = T // P
+PASSES = 2
+HALF = 512
+X_LOADS = ((0, 1), (1, 3), (4, 4), (8, 4), (12, 4))
+LAG = {'W': 0, 'T': 3, 'C': 3, 'QX': 4, 'Y0': 8, 'Y1': 8, 'SQ0': 8, 'SQ1': 8, 'Q2': 10, 'QQ': 10, 'PL0': 12, 'PL1': 11, 'AD0': 13, 'AD1': 13, 'SG': 14}
+ORDER = ['W', 'perm', 'AD1', 'Q2', 'T', 'AD0', 'PL0', 'QX', 'Y0', 'SG', 'QQ', 'C', 'SQ0', 'Y1', 'SQ1', 'PL1']
+WIDEN_ON_SCALAR = {0, 1, 5, 7, 9, 11, 13, 15}
+COPY_ON_VECTOR = {8, 11, 3, 4}
+PERMUTE_STEP = [0, 0, 0, 1]
+X_STEP = [0, 2, 3, 3, 6, 6, 8, 8, 10, 10, 12, 12, 13, 13, 18, 18]
+TINY = 2.0 ** -56
+
+
+def tile_centredsoftplusdivisivenormtransform_d1p_kernel(
+    tc, x_bytes, x_scale, w_words, w_scales, p, gamma_words, gamma_scales, beta, out
+):
+    nc = tc.nc
+    x_rows = x_bytes.rearrange("(p i) k -> p (i k)", i=TILES)
+    out_rows = out.rearrange("(p i) c -> p i c", i=TILES)
+
+    with ExitStack() as ctx:
+        keep = ctx.enter_context(tc.tile_pool(name="keep", bufs=1))
+        ring = ctx.enter_context(tc.tile_pool(name="ring", bufs=3))
+        psum = ctx.enter_context(tc.psum_pool(name="psum", bufs=1))
+        ctx.enter_context(tc.manual_schedule())
+
+        ident = keep.tile([P, P], F32)
+        make_identity(nc, ident[:])
+
+        w_sc = keep.tile([P, PASSES, C], U8, align_bytes=64)
+        g_sc = keep.tile([P, PASSES, C], U8, align_bytes=64)
+        nc.vector.memset(w_sc[:].rearrange("p g n -> p (g n)").bitcast(I32), 0)
+        nc.vector.memset(g_sc[:].rearrange("p g n -> p (g n)").bitcast(I32), 0)
+        tiny = keep.tile([P, 1], F32)
+        nc.vector.memset(tiny[:], TINY)
+        one = keep.tile([P, 1], F32)
+        nc.vector.memset(one[:], 1.0)
+        tenth = keep.tile([P, 1], F32)
+        nc.vector.tensor_scalar(out=tenth[:], in0=one[:], scalar1=0.1, scalar2=None, op0=ALU.mult)
+        warm = keep.tile([P, 1], F32)
+        nc.scalar.activation(out=warm[:], in_=one[:], func=ACT.Sigmoid)
+
+        def load_scales(plane, scales):
+            for q in range(4):
+                nc.sync.dma_start(
+                    out=plane[32 * q : 32 * q + 4, :, :].bitcast(I32),
+                    in_=scales[:, 4 * q : 4 * q + 4, :].rearrange("g r n -> r g n").bitcast(I32),
+                )
+
+        def load_words(dst, words, h):
+            cols = slice(2 * HALF * h, 2 * HALF * (h + 1))
+            nc.sync.dma_start(
+                out=dst[:, :, cols].bitcast(I32), in_=words[:, :, cols].rearrange("g p b -> p g b").bitcast(I32)
+            )
+
+        x_raw = {}
+
+        def load_x(first, count):
+            raw = keep.tile([P, count * D], U8, name="x_raw%d" % first)
+            nc.sync.dma_start(out=raw[:], in_=x_rows[:, first * D : (first + count) * D])
+            for j in range(count):
+                x_raw[first + j] = raw[:, j * D : (j + 1) * D]
+
+        w_wd = keep.tile([P, PASSES, 2 * C], U8, align_bytes=64)
+        g_wd = keep.tile([P, PASSES, 2 * C], U8, align_bytes=64)
+        xs = keep.tile([P, TILES * 8], F32)
+        p_cols = keep.tile([P, PASSES, 4], BF16)
+        beta_all = keep.tile([P, C], BF16)
+
+        load_scales(w_sc, w_scales)
+        load_words(w_wd, w_words, 0)
+        nc.sync.dma_start(out=xs[:], in_=x_scale.rearrange("(p i) j -> p (i j)", i=TILES))
+        load_x(*X_LOADS[0])
+        load_words(w_wd, w_words, 1)
+        load_x(*X_LOADS[1])
+        nc.sync.dma_start(out=p_cols[:], in_=p.rearrange("(g p t) -> p g t", p=P, t=4))
+        load_x(*X_LOADS[2])
+        load_scales(g_sc, gamma_scales)
+        load_words(g_wd, gamma_words, 0)
+        load_words(g_wd, gamma_words, 1)
+        nc.sync.dma_start(out=beta_all[:], in_=beta.partition_broadcast(P))
+        for first, count in X_LOADS[3:]:
+            load_x(first, count)
+
+        wp_wd = [keep.tile([P, PASSES, 2 * HALF], U8, align_bytes=64, name="wp_wd%d" % h) for h in range(2)]
+        wp_sc = [keep.tile([P, PASSES, HALF], U8, align_bytes=64, name="wp_sc%d" % h) for h in range(2)]
+        p_all = keep.tile([P, PASSES, P, 4], BF16)
+
+        def permute(k):
+            h, g = divmod(k, 2)
+            nc.vector.tensor_copy(
+                out=wp_wd[h][:, g, :].rearrange("p (t m b) -> p t m b", t=4, b=2),
+                in_=w_wd[:, g, 2 * HALF * h : 2 * HALF * (h + 1)].rearrange("p (m t b) -> p t m b", t=4, b=2),
+            )
+            nc.vector.tensor_copy(
+                out=wp_sc[h][:, g, :].rearrange("p (t m) -> p t m", t=4),
+                in_=w_sc[:, g, HALF * h : HALF * (h + 1)].rearrange("p (m t) -> p t m", t=4),
+            )
+
+        xb, xt, xg, xq, xq_sc, yt, sq, qb, qq, qq_sc, acc, neg, soft = ({} for n in range(13))
+
+        def widen(i):
+            xb[i] = ring.tile([P, D], BF16, tag="xb", name="xb", bufs=6)
+            for j in range(8):
+                cols = slice(P * j, P * (j + 1))
+                scale = xs[:, 8 * i + j : 8 * i + j + 1]
+                if i in WIDEN_ON_SCALAR:
+                    nc.scalar.activation(out=xb[i][:, cols], in_=x_raw[i][:, cols].bitcast(FP8), func=ACT.Copy, scale=scale)
+                else:
+                    nc.vector.tensor_scalar(
+                        out=xb[i][:, cols], in0=x_raw[i][:, cols].bitcast(FP8), scalar1=scale, scalar2=None, op0=ALU.mult
+                    )
+
+        def turn(i):
+            words = xb[i][:].bitcast(F32)
+            xt[i] = psum.tile([P, 4, P], F32, tag="xt", name="xt", bufs=2)
+            for g in range(PASSES):
+                for u in range(2):
+                    nc.tensor.transpose(xt[i][:, 2 * g + u, :], words[:, 256 * g + u : 256 * (g + 1) : 2], ident[:])
+
+        def copy_out(i):
+            xg[i] = ring.tile([P, D], BF16, tag="xg", name="xg", align_bytes=64, bufs=3)
+            dst = xg[i][:].bitcast(F32).rearrange("p (g r u) -> p g r u", g=PASSES, u=2)
+            src = xt[i][:].rearrange("p (g u) r -> p g r u", u=2)
+            if i in COPY_ON_VECTOR:
+                nc.vector.tensor_copy(out=dst, in_=src)
+            else:
+                nc.scalar.copy(out=dst, in_=src)
+
+        def quantize_x(i):
+            xq[i] = keep.tile([P, PASSES * P], U32, name="xq%d" % i, align_bytes=64)
+            xq_sc[i] = keep.tile([P, PASSES * P], U8, name="xq_sc%d" % i, align_bytes=64)
+            nc.vector.quantize_mx(out=xq[i][:].bitcast(FP8X4), scales=xq_sc[i][:], in_=xg[i][:])
+
+        def y_by_channel(i, h):
+            yt[i, h] = psum.tile([P, 4, P], F32, tag="yt", name="yt", bufs=3)
+            for t in range(4):
+                for g in range(PASSES):
+                    nc.tensor.matmul_mx(
+                        out=yt[i, h][:, t, :],
+                        lhsT=wp_wd[h][:, g, 2 * P * t : 2 * P * (t + 1)].bitcast(FP4X4),
+                        lhsT_scale=wp_sc[h][:, g, P * t : P * (t + 1)],
+                        rhs=xq[i][:, P * g : P * (g + 1)].bitcast(FP8X4),
+                        rhs_scale=xq_sc[i][:, P * g : P * (g + 1)],
+                        start=(g == 0),
+                        stop=(g == PASSES - 1),
+                    )
+
+        def square(i, h):
+            if i not in sq:
+                sq[i] = ring.tile([P, C], F32, tag="sq", name="sq", bufs=3)
+            nc.scalar.activation(
+                out=sq[i][:, HALF * h : HALF * (h + 1)].rearrange("p (n t) -> p n t", t=4),
+                in_=yt[i, h][:].rearrange("p t n -> p n t"),
+                func=ACT.Square,
+            )
+
+        def centre(i):
+            if i == 0:
+                for g in range(PASSES):
+                    nc.vector.tensor_copy(out=p_all[:, g, :, :], in_=p_cols[:, g : g + 1, :].to_broadcast([P, P, 4]))
+            qb[i] = ring.tile([P, C], BF16, tag="qb", name="qb", align_bytes=64, bufs=2)
+            nc.vector.scalar_tensor_tensor(
+                out=qb[i][:],
+                in0=sq[i][:],
+                scalar=-1.0,
+                in1=p_all[:].rearrange("p g n t -> p (g n t)"),
+                op0=ALU.add,
+                op1=ALU.mult,
+            )
+
+        def quantize_q(i):
+            qq[i] = ring.tile([P, PASSES * P], U32, tag="qq", name="qq", align_bytes=64, bufs=4)
+            qq_sc[i] = ring.tile([P, PASSES * P], U8, tag="qq_sc", name="qq_sc", align_bytes=64, bufs=4)
+            nc.vector.quantize_mx(out=qq[i][:].bitcast(FP8X4), scales=qq_sc[i][:], in_=qb[i][:])
+
+        def by_token(i, h, codes, scales, words, word_scales):
+            acc[i, h] = psum.tile([P, HALF], F32, tag="acc", name="acc", bufs=3)
+            for g in range(PASSES):
+                nc.tensor.matmul_mx(
+                    out=acc[i, h][:],
+                    lhsT=codes[:, P * g : P * (g + 1)].bitcast(FP8X4),
+                    lhsT_scale=scales[:, P * g : P * (g + 1)],
+                    rhs=words[:, g, 2 * HALF * h : 2 * HALF * (h + 1)].bitcast(FP4X4),
+                    rhs_scale=word_scales[:, g, HALF * h : HALF * (h + 1)],
+                    start=(g == 0),
+                    stop=(g == PASSES - 1),
+                )
+
+        def pool_product(i, h):
+            by_token(i, h, qq[i], qq_sc[i], g_wd, g_sc)
+
+        def add_beta(i, h):
+            if i not in neg:
+                neg[i] = keep.tile([P, C], F32, name="neg%d" % i)
+            cols = slice(HALF * h, HALF * (h + 1))
+            nc.vector.scalar_tensor_tensor(
+                out=neg[i][:, cols], in0=acc[i, h][:], scalar=-1.0, in1=beta_all[:, cols], op0=ALU.mult, op1=ALU.subtract
+            )
+
+        def sigmoid(i):
+            soft[i] = keep.tile([P, C], F32, name="soft%d" % i)
+            nc.scalar.activation(out=soft[i][:], in_=neg[i][:], func=ACT.Sigmoid)
+
+        stages = {
+            "W": widen,
+            "T": turn,
+            "C": copy_out,
+            "QX": quantize_x,
+            "Y0": lambda i: y_by_channel(i, 0),
+            "Y1": lambda i: y_by_channel(i, 1),
+            "SQ0": lambda i: square(i, 0),
+            "SQ1": lambda i: square(i, 1),
+            "Q2": centre,
+            "QQ": quantize_q,
+            "PL0": lambda i: pool_product(i, 0),
+            "PL1": lambda i: pool_product(i, 1),
+            "AD0": lambda i: add_beta(i, 0),
+            "AD1": lambda i: add_beta(i, 1),
+            "SG": sigmoid,
+        }
+        for step in range(TILES + max(LAG.values()) + max(X_STEP)):
+            for name in ORDER:
+                if name == "perm":
+                    for k in range(4):
+                        if PERMUTE_STEP[k] == step:
+                            permute(k)
+                    continue
+                for i in range(TILES):
+                    start = X_STEP[i] if name in ("W", "T", "C", "QX") else i
+                    if start + LAG[name] == step:
+                        stages[name](i)
+
+        for i in range(TILES):
+            nc.scalar.activation(out=soft[i][:], in_=soft[i][:], func=ACT.Ln, bias=tiny[:])
+            nc.vector.tensor_tensor(out=soft[i][:], in0=soft[i][:], in1=neg[i][:], op=ALU.min)
+
+        for i in range(TILES):
+            nc.scalar.activation(out=soft[i][:], in_=soft[i][:], func=ACT.Abs_reciprocal_sqrt, scale=-1.0, bias=tenth[:])
+            for h in range(2):
+                by_token(i, h, xq[i], xq_sc[i], w_wd, w_sc)
+            for h in range(2):
+                cols = slice(HALF * h, HALF * (h + 1))
+                nc.vector.tensor_tensor(out=neg[i][:, cols], in0=acc[i, h][:], in1=soft[i][:, cols], op=ALU.mult)
+            nc.sync.dma_start(out=out_rows[:, i, :], in_=neg[i][:])

@@ -21,13 +21,15 @@ P = 128
 TILES = T // P
 PASSES = 2
 HALF = 512
-X_LOADS = ((0, 1), (1, 3), (4, 4), (8, 4), (12, 4))
-LAG = {'W': 0, 'T': 3, 'C': 3, 'QX': 4, 'Y0': 8, 'Y1': 8, 'SQ0': 8, 'SQ1': 8, 'Q2': 10, 'QQ': 10, 'PL0': 12, 'PL1': 11, 'AD0': 13, 'AD1': 13, 'SG': 14}
-ORDER = ['W', 'perm', 'AD1', 'Q2', 'T', 'AD0', 'PL0', 'QX', 'Y0', 'SG', 'QQ', 'C', 'SQ0', 'Y1', 'SQ1', 'PL1']
-WIDEN_ON_SCALAR = {0, 1, 5, 7, 9, 11, 13, 15}
-COPY_ON_VECTOR = {8, 11, 3, 4}
-PERMUTE_STEP = [0, 0, 0, 1]
-X_STEP = [0, 2, 3, 3, 6, 6, 8, 8, 10, 10, 12, 12, 13, 13, 18, 18]
+X_LOADS = ((0, 2), (2, 2), (4, 4), (8, 4), (12, 4))
+LAG = {'W': 0, 'T': 1, 'C': 1, 'QX': 2, 'Y0': 5, 'Y1': 5, 'SQ0': 5, 'SQ1': 6, 'Q2': 7, 'QQ': 7, 'PL0': 8, 'PL1': 9, 'AD0': 9, 'AD1': 9, 'SG': 11}
+ORDER = ['Q2', 'AD0', 'QX', 'PL1', 'SQ1', 'SG', 'PL0', 'W', 'T', 'C', 'QQ', 'AD1', 'Y0', 'SQ0', 'Y1', 'perm']
+WIDEN_ON_SCALAR = {1, 2, 5, 8, 10, 11, 12, 13, 15}
+COPY_ON_VECTOR = {4, 5}
+PERMUTE_STEP = [2, 3, 2, 3]
+X_STEP = [1, 2, 3, 6, 6, 7, 7, 8, 8, 9, 9, 10, 10, 13, 16, 16]
+BANKS = {"xt": 2, "yt": 3, "acc": 3}
+ON_GPSIMD = (6, 12)
 TINY = 2.0 ** -56
 
 
@@ -57,12 +59,10 @@ def tile_centredsoftplusdivisivenormtransform_d1p_kernel(
         nc.vector.memset(one[:], 1.0)
         tenth = keep.tile([P, 1], F32)
         nc.vector.tensor_scalar(out=tenth[:], in0=one[:], scalar1=0.1, scalar2=None, op0=ALU.mult)
-        warm = keep.tile([P, 1], F32)
-        nc.scalar.activation(out=warm[:], in_=one[:], func=ACT.Sigmoid)
 
-        def load_scales(plane, scales):
+        def load_scales(queue, plane, scales):
             for q in range(4):
-                nc.sync.dma_start(
+                queue.dma_start(
                     out=plane[32 * q : 32 * q + 4, :, :].bitcast(I32),
                     in_=scales[:, 4 * q : 4 * q + 4, :].rearrange("g r n -> r g n").bitcast(I32),
                 )
@@ -87,7 +87,7 @@ def tile_centredsoftplusdivisivenormtransform_d1p_kernel(
         p_cols = keep.tile([P, PASSES, 4], BF16)
         beta_all = keep.tile([P, C], BF16)
 
-        load_scales(w_sc, w_scales)
+        load_scales(nc.scalar, w_sc, w_scales)
         load_words(w_wd, w_words, 0)
         nc.sync.dma_start(out=xs[:], in_=x_scale.rearrange("(p i) j -> p (i j)", i=TILES))
         load_x(*X_LOADS[0])
@@ -95,10 +95,12 @@ def tile_centredsoftplusdivisivenormtransform_d1p_kernel(
         load_x(*X_LOADS[1])
         nc.sync.dma_start(out=p_cols[:], in_=p.rearrange("(g p t) -> p g t", p=P, t=4))
         load_x(*X_LOADS[2])
-        load_scales(g_sc, gamma_scales)
+        load_scales(nc.sync, g_sc, gamma_scales)
         load_words(g_wd, gamma_words, 0)
         load_words(g_wd, gamma_words, 1)
         nc.sync.dma_start(out=beta_all[:], in_=beta.partition_broadcast(P))
+        warm = keep.tile([P, 1], F32)
+        nc.scalar.activation(out=warm[:], in_=one[:], func=ACT.Sigmoid)
         for first, count in X_LOADS[3:]:
             load_x(first, count)
 
@@ -194,8 +196,8 @@ def tile_centredsoftplusdivisivenormtransform_d1p_kernel(
             qq_sc[i] = ring.tile([P, PASSES * P], U8, tag="qq_sc", name="qq_sc", align_bytes=64, bufs=4)
             nc.vector.quantize_mx(out=qq[i][:].bitcast(FP8X4), scales=qq_sc[i][:], in_=qb[i][:])
 
-        def by_token(i, h, codes, scales, words, word_scales):
-            acc[i, h] = psum.tile([P, HALF], F32, tag="acc", name="acc", bufs=3)
+        def by_token(i, h, codes, scales, words, word_scales, tag="acc"):
+            acc[i, h] = psum.tile([P, HALF], F32, tag=tag, name=tag, bufs=BANKS[tag])
             for g in range(PASSES):
                 nc.tensor.matmul_mx(
                     out=acc[i, h][:],
@@ -251,15 +253,56 @@ def tile_centredsoftplusdivisivenormtransform_d1p_kernel(
                     if start + LAG[name] == step:
                         stages[name](i)
 
+        tags = [tag for tag in BANKS for n in range(BANKS[tag])]
+        halves = [(i, h) for i in ON_GPSIMD for h in range(2)]
+        halves += [(i, h) for i in range(TILES) if i not in ON_GPSIMD for h in range(2)]
+        made = []
+
+        def next_y():
+            if len(made) < len(halves):
+                i, h = halves[len(made)]
+                by_token(i, h, xq[i], xq_sc[i], w_wd, w_sc, tag=tags[len(made) % len(tags)])
+                made.append((i, h))
+
+        for n in range(len(tags)):
+            next_y()
+        y_sb = {}
+        for i in ON_GPSIMD:
+            y_sb[i] = ring.tile([P, C], F32, tag="sq", name="sq", bufs=3)
+            for h in range(2):
+                nc.vector.tensor_copy(out=y_sb[i][:, HALF * h : HALF * (h + 1)], in_=acc[i, h][:])
+                next_y()
+
         for i in range(TILES):
             nc.scalar.activation(out=soft[i][:], in_=soft[i][:], func=ACT.Ln, bias=tiny[:])
             nc.vector.tensor_tensor(out=soft[i][:], in0=soft[i][:], in1=neg[i][:], op=ALU.min)
 
+        late = []
         for i in range(TILES):
-            nc.scalar.activation(out=soft[i][:], in_=soft[i][:], func=ACT.Abs_reciprocal_sqrt, scale=-1.0, bias=tenth[:])
-            for h in range(2):
-                by_token(i, h, xq[i], xq_sc[i], w_wd, w_sc)
-            for h in range(2):
-                cols = slice(HALF * h, HALF * (h + 1))
-                nc.vector.tensor_tensor(out=neg[i][:, cols], in0=acc[i, h][:], in1=soft[i][:, cols], op=ALU.mult)
-            nc.sync.dma_start(out=out_rows[:, i, :], in_=neg[i][:])
+            pieces = 4 if i == TILES - 1 else 1
+            width = C // pieces
+            for n in range(pieces):
+                cols = slice(width * n, width * (n + 1))
+                nc.scalar.activation(
+                    out=soft[i][:, cols], in_=soft[i][:, cols], func=ACT.Abs_reciprocal_sqrt, scale=-1.0, bias=tenth[:]
+                )
+            if i in ON_GPSIMD:
+                nc.gpsimd.tensor_tensor(out=neg[i][:], in0=y_sb[i][:], in1=soft[i][:], op=ALU.mult)
+                late.append(i)
+                continue
+            width = min(width, HALF)
+            for n in range(C // width):
+                cols = slice(width * n, width * (n + 1))
+                h, start = divmod(width * n, HALF)
+                nc.vector.tensor_tensor(
+                    out=neg[i][:, cols], in0=acc[i, h][:, start : start + width], in1=soft[i][:, cols], op=ALU.mult
+                )
+                if start + width == HALF:
+                    next_y()
+                if pieces > 1:
+                    nc.sync.dma_start(out=out_rows[:, i, cols], in_=neg[i][:, cols])
+            if pieces == 1:
+                nc.sync.dma_start(out=out_rows[:, i, :], in_=neg[i][:])
+            if late and i == late[0] + 2:
+                nc.sync.dma_start(out=out_rows[:, late[0], :], in_=neg[late[0]][:])
+                late.remove(late[0])

@@ -22,14 +22,14 @@ TILES = T // P
 PASSES = 2
 HALF = 512
 X_LOADS = ((0, 2), (2, 2), (4, 4), (8, 4), (12, 4))
-LAG = {'W': 0, 'T': 1, 'C': 1, 'QX': 2, 'Y0': 5, 'Y1': 5, 'SQ0': 5, 'SQ1': 6, 'Q2': 7, 'QQ': 7, 'PL0': 8, 'PL1': 9, 'AD0': 9, 'AD1': 9, 'SG': 11}
-ORDER = ['Q2', 'AD0', 'QX', 'PL1', 'SQ1', 'SG', 'PL0', 'W', 'T', 'C', 'QQ', 'AD1', 'Y0', 'SQ0', 'Y1', 'perm']
-WIDEN_ON_SCALAR = {1, 2, 5, 8, 10, 11, 12, 13, 15}
-COPY_ON_VECTOR = {4, 5}
-PERMUTE_STEP = [2, 3, 2, 3]
-X_STEP = [1, 2, 3, 6, 6, 7, 7, 8, 8, 9, 9, 10, 10, 13, 16, 16]
-BANKS = {"xt": 2, "yt": 3, "acc": 3}
-ON_GPSIMD = (6, 12)
+LAG = {'W': 0, 'T': 2, 'C': 2, 'QX': 3, 'Y0': 8, 'Y1': 8, 'SQ0': 8, 'SQ1': 9, 'Q2': 10, 'QQ': 10, 'PL0': 12, 'PL1': 11, 'AD0': 12, 'AD1': 12, 'SG': 14}
+ORDER = ['PL0', 'T', 'Q2', 'PL1', 'AD1', 'SQ1', 'Y0', 'QX', 'perm', 'Y1', 'QQ', 'AD0', 'C', 'SG', 'W', 'SQ0']
+WIDEN_ON_SCALAR = {1, 2, 3, 4, 8, 10, 11, 12, 13}
+COPY_ON_VECTOR = {1, 7}
+PERMUTE_STEP = [1, 1, 3, 3]
+X_STEP = [0, 1, 6, 7, 7, 8, 8, 11, 11, 11, 12, 12, 12, 13, 13, 13]
+BANKS = {"xt": 3, "yt": 2, "acc": 3}
+ON_GPSIMD = ()
 TINY = 2.0 ** -56
 
 
@@ -46,17 +46,16 @@ def tile_centredsoftplusdivisivenormtransform_d1p_kernel(
         psum = ctx.enter_context(tc.psum_pool(name="psum", bufs=1))
         ctx.enter_context(tc.manual_schedule())
 
-        ident = keep.tile([P, P], F32)
-        make_identity(nc, ident[:])
-
         w_sc = keep.tile([P, PASSES, C], U8, align_bytes=64)
         g_sc = keep.tile([P, PASSES, C], U8, align_bytes=64)
-        nc.vector.memset(w_sc[:].rearrange("p g n -> p (g n)").bitcast(I32), 0)
+        nc.gpsimd.memset(w_sc[:].rearrange("p g n -> p (g n)").bitcast(I32), 0)
+        ident = keep.tile([P, P], F32)
+        make_identity(nc, ident[:])
+        one = keep.tile([P, 1], F32)
+        nc.vector.memset(one[:], 1.0)
         nc.vector.memset(g_sc[:].rearrange("p g n -> p (g n)").bitcast(I32), 0)
         tiny = keep.tile([P, 1], F32)
         nc.vector.memset(tiny[:], TINY)
-        one = keep.tile([P, 1], F32)
-        nc.vector.memset(one[:], 1.0)
         tenth = keep.tile([P, 1], F32)
         nc.vector.tensor_scalar(out=tenth[:], in0=one[:], scalar1=0.1, scalar2=None, op0=ALU.mult)
 
@@ -87,10 +86,12 @@ def tile_centredsoftplusdivisivenormtransform_d1p_kernel(
         p_cols = keep.tile([P, PASSES, 4], BF16)
         beta_all = keep.tile([P, C], BF16)
 
-        load_scales(nc.scalar, w_sc, w_scales)
-        load_words(w_wd, w_words, 0)
+        warm = keep.tile([P, 1], F32)
+        nc.scalar.activation(out=warm[:], in_=one[:], func=ACT.Sigmoid)
         nc.sync.dma_start(out=xs[:], in_=x_scale.rearrange("(p i) j -> p (i j)", i=TILES))
         load_x(*X_LOADS[0])
+        load_words(w_wd, w_words, 0)
+        load_scales(nc.sync, w_sc, w_scales)
         load_words(w_wd, w_words, 1)
         load_x(*X_LOADS[1])
         nc.sync.dma_start(out=p_cols[:], in_=p.rearrange("(g p t) -> p g t", p=P, t=4))
@@ -99,8 +100,6 @@ def tile_centredsoftplusdivisivenormtransform_d1p_kernel(
         load_words(g_wd, gamma_words, 0)
         load_words(g_wd, gamma_words, 1)
         nc.sync.dma_start(out=beta_all[:], in_=beta.partition_broadcast(P))
-        warm = keep.tile([P, 1], F32)
-        nc.scalar.activation(out=warm[:], in_=one[:], func=ACT.Sigmoid)
         for first, count in X_LOADS[3:]:
             load_x(first, count)
 
@@ -135,7 +134,7 @@ def tile_centredsoftplusdivisivenormtransform_d1p_kernel(
 
         def turn(i):
             words = xb[i][:].bitcast(F32)
-            xt[i] = psum.tile([P, 4, P], F32, tag="xt", name="xt", bufs=2)
+            xt[i] = psum.tile([P, 4, P], F32, tag="xt", name="xt", bufs=3)
             for g in range(PASSES):
                 for u in range(2):
                     nc.tensor.transpose(xt[i][:, 2 * g + u, :], words[:, 256 * g + u : 256 * (g + 1) : 2], ident[:])
@@ -155,7 +154,7 @@ def tile_centredsoftplusdivisivenormtransform_d1p_kernel(
             nc.vector.quantize_mx(out=xq[i][:].bitcast(FP8X4), scales=xq_sc[i][:], in_=xg[i][:])
 
         def y_by_channel(i, h):
-            yt[i, h] = psum.tile([P, 4, P], F32, tag="yt", name="yt", bufs=3)
+            yt[i, h] = psum.tile([P, 4, P], F32, tag="yt", name="yt", bufs=2)
             for t in range(4):
                 for g in range(PASSES):
                     nc.tensor.matmul_mx(
@@ -222,7 +221,12 @@ def tile_centredsoftplusdivisivenormtransform_d1p_kernel(
 
         def sigmoid(i):
             soft[i] = keep.tile([P, C], F32, name="soft%d" % i)
-            nc.scalar.activation(out=soft[i][:], in_=neg[i][:], func=ACT.Sigmoid)
+            if i < TILES - 1:
+                nc.scalar.activation(out=soft[i][:], in_=neg[i][:], func=ACT.Sigmoid)
+                return
+            for h in (1, 0):
+                cols = slice(HALF * h, HALF * (h + 1))
+                nc.scalar.activation(out=soft[i][:, cols], in_=neg[i][:, cols], func=ACT.Sigmoid)
 
         stages = {
             "W": widen,
@@ -279,7 +283,7 @@ def tile_centredsoftplusdivisivenormtransform_d1p_kernel(
 
         late = []
         for i in range(TILES):
-            pieces = 4 if i == TILES - 1 else 1
+            pieces = 4 if i == TILES - 1 else 2 if i == 0 else 1
             width = C // pieces
             for n in range(pieces):
                 cols = slice(width * n, width * (n + 1))

from contextlib import ExitStack

import concourse.mybir as mybir
from concourse.masks import make_identity

T, D, C = 2048, 1024, 1024
FLOPS = 2 * T * D * C + 2 * T * C * C

F32 = mybir.dt.float32
BF16 = mybir.dt.bfloat16
U32 = mybir.dt.uint32
I32 = mybir.dt.int32
U8 = mybir.dt.uint8
FP8 = mybir.dt.float8_e4m3fn
FP8X4 = mybir.dt.float8_e4m3fn_x4
FP4X4 = mybir.dt.float4_e2m1fn_x4
ALU = mybir.AluOpType
ACT = mybir.ActivationFunctionType

P = 128
TILES = T // P
PASSES = 2
HALF = 512
X_LOADS = ((0, 2), (2, 2), (4, 4), (8, 4), (12, 4))
LAG = {'W': 0, 'T': 2, 'C': 2, 'QX': 3, 'Y0': 8, 'Y1': 8, 'SQ0': 8, 'SQ1': 9, 'Q2': 10, 'QQ': 10, 'PL0': 12, 'PL1': 11, 'AD0': 12, 'AD1': 12, 'SG': 14}
ORDER = ['PL0', 'T', 'Q2', 'PL1', 'AD1', 'SQ1', 'Y0', 'QX', 'perm', 'Y1', 'QQ', 'AD0', 'C', 'SG', 'W', 'SQ0']
WIDEN_ON_SCALAR = {1, 2, 3, 4, 8, 10, 11, 12, 13}
COPY_ON_VECTOR = {1, 7}
PERMUTE_STEP = [1, 1, 3, 3]
X_STEP = [0, 1, 6, 7, 7, 8, 8, 11, 11, 11, 12, 12, 12, 13, 13, 13]
BANKS = {"xt": 3, "yt": 2, "acc": 3}
ON_GPSIMD = ()
TINY = 2.0 ** -56


def tile_centredsoftplusdivisivenormtransform_d1p_kernel(
    tc, x_bytes, x_scale, w_words, w_scales, p, gamma_words, gamma_scales, beta, out
):
    nc = tc.nc
    x_rows = x_bytes.rearrange("(p i) k -> p (i k)", i=TILES)
    out_rows = out.rearrange("(p i) c -> p i c", i=TILES)

    with ExitStack() as ctx:
        keep = ctx.enter_context(tc.tile_pool(name="keep", bufs=1))
        ring = ctx.enter_context(tc.tile_pool(name="ring", bufs=3))
        psum = ctx.enter_context(tc.psum_pool(name="psum", bufs=1))
        ctx.enter_context(tc.manual_schedule())

        w_sc = keep.tile([P, PASSES, C], U8, align_bytes=64)
        g_sc = keep.tile([P, PASSES, C], U8, align_bytes=64)
        nc.gpsimd.memset(w_sc[:].rearrange("p g n -> p (g n)").bitcast(I32), 0)
        ident = keep.tile([P, P], F32)
        make_identity(nc, ident[:])
        one = keep.tile([P, 1], F32)
        nc.vector.memset(one[:], 1.0)
        nc.vector.memset(g_sc[:].rearrange("p g n -> p (g n)").bitcast(I32), 0)
        tiny = keep.tile([P, 1], F32)
        nc.vector.memset(tiny[:], TINY)
        tenth = keep.tile([P, 1], F32)
        nc.vector.tensor_scalar(out=tenth[:], in0=one[:], scalar1=0.1, scalar2=None, op0=ALU.mult)

        def load_scales(queue, plane, scales):
            for q in range(4):
                queue.dma_start(
                    out=plane[32 * q : 32 * q + 4, :, :].bitcast(I32),
                    in_=scales[:, 4 * q : 4 * q + 4, :].rearrange("g r n -> r g n").bitcast(I32),
                )

        def load_words(dst, words, h):
            cols = slice(2 * HALF * h, 2 * HALF * (h + 1))
            nc.sync.dma_start(
                out=dst[:, :, cols].bitcast(I32), in_=words[:, :, cols].rearrange("g p b -> p g b").bitcast(I32)
            )

        x_raw = {}

        def load_x(first, count):
            raw = keep.tile([P, count * D], U8, name="x_raw%d" % first)
            nc.sync.dma_start(out=raw[:], in_=x_rows[:, first * D : (first + count) * D])
            for j in range(count):
                x_raw[first + j] = raw[:, j * D : (j + 1) * D]

        w_wd = keep.tile([P, PASSES, 2 * C], U8, align_bytes=64)
        g_wd = keep.tile([P, PASSES, 2 * C], U8, align_bytes=64)
        xs = keep.tile([P, TILES * 8], F32)
        p_cols = keep.tile([P, PASSES, 4], BF16)
        beta_all = keep.tile([P, C], BF16)

        warm = keep.tile([P, 1], F32)
        nc.scalar.activation(out=warm[:], in_=one[:], func=ACT.Sigmoid)
        nc.sync.dma_start(out=xs[:], in_=x_scale.rearrange("(p i) j -> p (i j)", i=TILES))
        load_x(*X_LOADS[0])
        load_words(w_wd, w_words, 0)
        load_scales(nc.sync, w_sc, w_scales)
        load_words(w_wd, w_words, 1)
        load_x(*X_LOADS[1])
        nc.sync.dma_start(out=p_cols[:], in_=p.rearrange("(g p t) -> p g t", p=P, t=4))
        load_x(*X_LOADS[2])
        load_scales(nc.sync, g_sc, gamma_scales)
        load_words(g_wd, gamma_words, 0)
        load_words(g_wd, gamma_words, 1)
        nc.sync.dma_start(out=beta_all[:], in_=beta.partition_broadcast(P))
        for first, count in X_LOADS[3:]:
            load_x(first, count)

        wp_wd = [keep.tile([P, PASSES, 2 * HALF], U8, align_bytes=64, name="wp_wd%d" % h) for h in range(2)]
        wp_sc = [keep.tile([P, PASSES, HALF], U8, align_bytes=64, name="wp_sc%d" % h) for h in range(2)]
        p_all = keep.tile([P, PASSES, P, 4], BF16)

        def permute(k):
            h, g = divmod(k, 2)
            nc.vector.tensor_copy(
                out=wp_wd[h][:, g, :].rearrange("p (t m b) -> p t m b", t=4, b=2),
                in_=w_wd[:, g, 2 * HALF * h : 2 * HALF * (h + 1)].rearrange("p (m t b) -> p t m b", t=4, b=2),
            )
            nc.vector.tensor_copy(
                out=wp_sc[h][:, g, :].rearrange("p (t m) -> p t m", t=4),
                in_=w_sc[:, g, HALF * h : HALF * (h + 1)].rearrange("p (m t) -> p t m", t=4),
            )

        xb, xt, xg, xq, xq_sc, yt, sq, qb, qq, qq_sc, acc, neg, soft = ({} for n in range(13))

        def widen(i):
            xb[i] = ring.tile([P, D], BF16, tag="xb", name="xb", bufs=6)
            for j in range(8):
                cols = slice(P * j, P * (j + 1))
                scale = xs[:, 8 * i + j : 8 * i + j + 1]
                if i in WIDEN_ON_SCALAR:
                    nc.scalar.activation(out=xb[i][:, cols], in_=x_raw[i][:, cols].bitcast(FP8), func=ACT.Copy, scale=scale)
                else:
                    nc.vector.tensor_scalar(
                        out=xb[i][:, cols], in0=x_raw[i][:, cols].bitcast(FP8), scalar1=scale, scalar2=None, op0=ALU.mult
                    )

        def turn(i):
            words = xb[i][:].bitcast(F32)
            xt[i] = psum.tile([P, 4, P], F32, tag="xt", name="xt", bufs=3)
            for g in range(PASSES):
                for u in range(2):
                    nc.tensor.transpose(xt[i][:, 2 * g + u, :], words[:, 256 * g + u : 256 * (g + 1) : 2], ident[:])

        def copy_out(i):
            xg[i] = ring.tile([P, D], BF16, tag="xg", name="xg", align_bytes=64, bufs=3)
            dst = xg[i][:].bitcast(F32).rearrange("p (g r u) -> p g r u", g=PASSES, u=2)
            src = xt[i][:].rearrange("p (g u) r -> p g r u", u=2)
            if i in COPY_ON_VECTOR:
                nc.vector.tensor_copy(out=dst, in_=src)
            else:
                nc.scalar.copy(out=dst, in_=src)

        def quantize_x(i):
            xq[i] = keep.tile([P, PASSES * P], U32, name="xq%d" % i, align_bytes=64)
            xq_sc[i] = keep.tile([P, PASSES * P], U8, name="xq_sc%d" % i, align_bytes=64)
            nc.vector.quantize_mx(out=xq[i][:].bitcast(FP8X4), scales=xq_sc[i][:], in_=xg[i][:])

        def y_by_channel(i, h):
            yt[i, h] = psum.tile([P, 4, P], F32, tag="yt", name="yt", bufs=2)
            for t in range(4):
                for g in range(PASSES):
                    nc.tensor.matmul_mx(
                        out=yt[i, h][:, t, :],
                        lhsT=wp_wd[h][:, g, 2 * P * t : 2 * P * (t + 1)].bitcast(FP4X4),
                        lhsT_scale=wp_sc[h][:, g, P * t : P * (t + 1)],
                        rhs=xq[i][:, P * g : P * (g + 1)].bitcast(FP8X4),
                        rhs_scale=xq_sc[i][:, P * g : P * (g + 1)],
                        start=(g == 0),
                        stop=(g == PASSES - 1),
                    )

        def square(i, h):
            if i not in sq:
                sq[i] = ring.tile([P, C], F32, tag="sq", name="sq", bufs=3)
            nc.scalar.activation(
                out=sq[i][:, HALF * h : HALF * (h + 1)].rearrange("p (n t) -> p n t", t=4),
                in_=yt[i, h][:].rearrange("p t n -> p n t"),
                func=ACT.Square,
            )

        def centre(i):
            if i == 0:
                for g in range(PASSES):
                    nc.vector.tensor_copy(out=p_all[:, g, :, :], in_=p_cols[:, g : g + 1, :].to_broadcast([P, P, 4]))
            qb[i] = ring.tile([P, C], BF16, tag="qb", name="qb", align_bytes=64, bufs=2)
            nc.vector.scalar_tensor_tensor(
                out=qb[i][:],
                in0=sq[i][:],
                scalar=-1.0,
                in1=p_all[:].rearrange("p g n t -> p (g n t)"),
                op0=ALU.add,
                op1=ALU.mult,
            )

        def quantize_q(i):
            qq[i] = ring.tile([P, PASSES * P], U32, tag="qq", name="qq", align_bytes=64, bufs=4)
            qq_sc[i] = ring.tile([P, PASSES * P], U8, tag="qq_sc", name="qq_sc", align_bytes=64, bufs=4)
            nc.vector.quantize_mx(out=qq[i][:].bitcast(FP8X4), scales=qq_sc[i][:], in_=qb[i][:])

        def by_token(i, h, codes, scales, words, word_scales, tag="acc"):
            acc[i, h] = psum.tile([P, HALF], F32, tag=tag, name=tag, bufs=BANKS[tag])
            for g in range(PASSES):
                nc.tensor.matmul_mx(
                    out=acc[i, h][:],
                    lhsT=codes[:, P * g : P * (g + 1)].bitcast(FP8X4),
                    lhsT_scale=scales[:, P * g : P * (g + 1)],
                    rhs=words[:, g, 2 * HALF * h : 2 * HALF * (h + 1)].bitcast(FP4X4),
                    rhs_scale=word_scales[:, g, HALF * h : HALF * (h + 1)],
                    start=(g == 0),
                    stop=(g == PASSES - 1),
                )

        def pool_product(i, h):
            by_token(i, h, qq[i], qq_sc[i], g_wd, g_sc)

        def add_beta(i, h):
            if i not in neg:
                neg[i] = keep.tile([P, C], F32, name="neg%d" % i)
            cols = slice(HALF * h, HALF * (h + 1))
            nc.vector.scalar_tensor_tensor(
                out=neg[i][:, cols], in0=acc[i, h][:], scalar=-1.0, in1=beta_all[:, cols], op0=ALU.mult, op1=ALU.subtract
            )

        def sigmoid(i):
            soft[i] = keep.tile([P, C], F32, name="soft%d" % i)
            if i < TILES - 1:
                nc.scalar.activation(out=soft[i][:], in_=neg[i][:], func=ACT.Sigmoid)
                return
            for h in (1, 0):
                cols = slice(HALF * h, HALF * (h + 1))
                nc.scalar.activation(out=soft[i][:, cols], in_=neg[i][:, cols], func=ACT.Sigmoid)

        stages = {
            "W": widen,
            "T": turn,
            "C": copy_out,
            "QX": quantize_x,
            "Y0": lambda i: y_by_channel(i, 0),
            "Y1": lambda i: y_by_channel(i, 1),
            "SQ0": lambda i: square(i, 0),
            "SQ1": lambda i: square(i, 1),
            "Q2": centre,
            "QQ": quantize_q,
            "PL0": lambda i: pool_product(i, 0),
            "PL1": lambda i: pool_product(i, 1),
            "AD0": lambda i: add_beta(i, 0),
            "AD1": lambda i: add_beta(i, 1),
            "SG": sigmoid,
        }
        for step in range(TILES + max(LAG.values()) + max(X_STEP)):
            for name in ORDER:
                if name == "perm":
                    for k in range(4):
                        if PERMUTE_STEP[k] == step:
                            permute(k)
                    continue
                for i in range(TILES):
                    start = X_STEP[i] if name in ("W", "T", "C", "QX") else i
                    if start + LAG[name] == step:
                        stages[name](i)

        tags = [tag for tag in BANKS for n in range(BANKS[tag])]
        halves = [(i, h) for i in ON_GPSIMD for h in range(2)]
        halves += [(i, h) for i in range(TILES) if i not in ON_GPSIMD for h in range(2)]
        made = []

        def next_y():
            if len(made) < len(halves):
                i, h = halves[len(made)]
                by_token(i, h, xq[i], xq_sc[i], w_wd, w_sc, tag=tags[len(made) % len(tags)])
                made.append((i, h))

        for n in range(len(tags)):
            next_y()
        y_sb = {}
        for i in ON_GPSIMD:
            y_sb[i] = ring.tile([P, C], F32, tag="sq", name="sq", bufs=3)
            for h in range(2):
                nc.vector.tensor_copy(out=y_sb[i][:, HALF * h : HALF * (h + 1)], in_=acc[i, h][:])
                next_y()

        for i in range(TILES):
            nc.scalar.activation(out=soft[i][:], in_=soft[i][:], func=ACT.Ln, bias=tiny[:])
            nc.vector.tensor_tensor(out=soft[i][:], in0=soft[i][:], in1=neg[i][:], op=ALU.min)

        late = []
        for i in range(TILES):
            pieces = 4 if i == TILES - 1 else 2 if i == 0 else 1
            width = C // pieces
            for n in range(pieces):
                cols = slice(width * n, width * (n + 1))
                nc.scalar.activation(
                    out=soft[i][:, cols], in_=soft[i][:, cols], func=ACT.Abs_reciprocal_sqrt, scale=-1.0, bias=tenth[:]
                )
            if i in ON_GPSIMD:
                nc.gpsimd.tensor_tensor(out=neg[i][:], in0=y_sb[i][:], in1=soft[i][:], op=ALU.mult)
                late.append(i)
                continue
            width = min(width, HALF)
            for n in range(C // width):
                cols = slice(width * n, width * (n + 1))
                h, start = divmod(width * n, HALF)
                nc.vector.tensor_tensor(
                    out=neg[i][:, cols], in0=acc[i, h][:, start : start + width], in1=soft[i][:, cols], op=ALU.mult
                )
                if start + width == HALF:
                    next_y()
                if pieces > 1:
                    nc.sync.dma_start(out=out_rows[:, i, cols], in_=neg[i][:, cols])
            if pieces == 1:
                nc.sync.dma_start(out=out_rows[:, i, :], in_=neg[i][:])
            if late and i == late[0] + 2:
                nc.sync.dma_start(out=out_rows[:, late[0], :], in_=neg[late[0]][:])
                late.remove(late[0])
